import numpy as np, ml_dtypes
CORES = [4,20,36,52,68,84,100,116,132,148,164,180,196,212,228,244]
N = 16
KB, QP = 1, 128
MEM = [3,10,11]
WID = [32,32,96,64,112,112,64,112,48,16,16,80,64,16,16,128]
def setup_inputs(rng):
    return {"q": rng.standard_normal((N, 128, QP), dtype=np.float32).astype(ml_dtypes.bfloat16), "k": rng.standard_normal((N, 128, KB * 128), dtype=np.float32).astype(ml_dtypes.bfloat16), "v": rng.standard_normal((N, 128, KB * 128), dtype=np.float32).astype(ml_dtypes.bfloat16)}
def setup_inputs_big(rng):
    d = setup_inputs(rng)
    for k in ("q", "k", "v"): d[k] = (d[k].astype(np.float32) * 1024.0).astype(d[k].dtype)
    return d
def setup_inputs_small(rng):
    d = setup_inputs(rng)
    for k in ("q", "k", "v"): d[k] = (d[k].astype(np.float32) * (1 / 1024.0)).astype(d[k].dtype)
    return d
def setup_inputs_apart(rng):
    d = setup_inputs(rng)
    f = (10.0 ** rng.permutation(np.linspace(-1.5, 1.5, N))).astype(np.float32).reshape(N, 1, 1)
    for k in ("q", "k", "v"): d[k] = (d[k].astype(np.float32) * f).astype(d[k].dtype)
    return d
def whole(q, k, v):
    Q, K, V = q.astype(np.float64), k.astype(np.float64), v.astype(np.float64)
    y = np.zeros((N, 128, QP))
    for r in range(N):
        for j in MEM:
            for b in range(KB):
                S = np.maximum(K[j][:, 128 * b:128 * b + 128].T @ Q[r], 0.0)
                y[r] += V[j][:, 128 * b:128 * b + 128].T @ S
    return {"y": y.astype(ml_dtypes.bfloat16 if q.dtype != np.float64 else np.float64)}
def reference(q, k, v):
    o = whole(q, k, v)["y"].copy()
    for r in range(N):
        o[r][:, WID[r]:] = np.nan
    return {"y": o}

@@ -1,0 +1,159 @@
+from concourse.bass import DstId, RemoteDMATransfer
+from concourse.mybir import AluOpType
+
+NCOL = 512
+NMEM = 3
+SLOT = 256
+
+SCRATCH = {
+    "kv": ("sbuf", [128, NMEM * SLOT], "bfloat16"),
+    "qs": ("sbuf", [128, NCOL], "bfloat16"),
+    "zero": ("sbuf", [128, NCOL], "float32"),
+    "sr": ("sbuf", [128, NMEM * NCOL], "bfloat16"),
+    "ys": ("sbuf", [128, NCOL], "bfloat16"),
+    "sp0": ("psum", [128, NCOL], "float32"),
+    "sp1": ("psum", [128, NCOL], "float32"),
+    "sp2": ("psum", [128, NCOL], "float32"),
+    "op": ("psum", [128, NCOL], "float32"),
+}
+SEMAPHORES = ["kv0", "kv1", "kv2", "qin", "ldq", "sent", "yin", "st", "zf",
+              "s10", "s11", "s12", "rl0", "rl1", "rl2", "od", "yr"]
+
+Q_ENGINES = 4
+
+
+def _plan(T):
+    mem, wid = list(T.tables["MEM"]), list(T.tables["WID"])
+    clients = sorted([r for r in range(len(T.cores)) if r not in mem], key=lambda r: (-wid[r], r))
+    base, extra = divmod(len(clients), len(mem))
+    servers = sorted(mem, key=lambda r: (wid[r], r))
+    plan, p = {}, 0
+    for i, srv in enumerate(servers):
+        size = base + (1 if i >= len(mem) - extra else 0)
+        order = sorted(clients[p:p + size], key=lambda r: (wid[r], r))
+        p += size
+        off, c = {}, 0
+        for r in order + [srv]:
+            off[r] = c
+            c += wid[r]
+        assert c <= NCOL
+        plan[srv] = (order, off, c)
+    return plan
+
+
+def _batches(order, wid, neng):
+    out, rest = [], list(order)
+    while rest:
+        b = 1
+        while b * 2 <= min(len(rest), neng):
+            b *= 2
+        out.append([(r, neng // b) for r in rest[len(rest) - b:]])
+        rest = rest[:len(rest) - b]
+    return out
+
+
+def _bits(mask):
+    return [e for e in range(16) if (mask >> e) & 1]
+
+
+def _mask(bits):
+    m = 0
+    for e in bits:
+        m |= 1 << e
+    return m
+
+
+def rank_program(g, core, T, topo):
+    rank = T.rank_of(core)
+    if rank is None:
+        return
+    mem, wid, sem = list(T.tables["MEM"]), list(T.tables["WID"]), T.sem
+    plan = _plan(T)
+    w = wid[rank]
+
+    def dst_id(d):
+        rid, pid = topo.addr(d, core)
+        return DstId(rid=rid, pnc=pid)
+
+    if rank not in mem:
+        srv = [s for s in plan if rank in plan[s][0]][0]
+        order, off, _ = plan[srv]
+        sc = T.cores[srv]
+        g.sync.dma_start(T.qs[:, 0:w], T.q[:, 0:w]).then_inc(sem.ldq, 16)
+        allowed = _bits(topo.mask(core, sc))
+        eng = allowed[::len(allowed) // Q_ENGINES][:Q_ENGINES]
+        rid, pid = topo.addr(sc, core)
+        g.wait_ge(sem.ldq, 16)
+        g.remote_dma(out_ap=T.qs[:, off[rank]:off[rank] + w], in_ap=T.qs[:, 0:w], remote_sem=sem.qin, local_sem=sem.sent,
+                     pid=pid, routing_id=rid, dma_engine_mask=_mask(eng))
+        g.wait_ge(sem.sent, len(eng))
+        back = len(_bits(topo.mask(sc, core)))
+        mine = [n for b in _batches(order, wid, back) for (r, n) in b if r == rank][0]
+        g.sync.wait_ge(sem.yin, mine)
+        g.sync.dma_start(T.y[:, 0:w], T.ys[:, 0:w]).then_inc(sem.st, 16)
+        g.sync.wait_ge(sem.st, 16)
+        return
+
+    order, off, n = plan[rank]
+    ns = len(mem)
+    i = mem.index(rank)
+    kvsem = [sem["kv%d" % m] for m in range(ns)]
+    te, ve = g.tensor, g.vector
+    k_of = lambda m: T.kv[:, m * SLOT:m * SLOT + 128]
+    v_of = lambda m: T.kv[:, m * SLOT + 128:(m + 1) * SLOT]
+    slot = T.kv[:, i * SLOT:(i + 1) * SLOT]
+
+    g.sync.dma_start(k_of(i), T.k[:, :]).then_inc(kvsem[i], 16)
+    g.scalar.dma_start(v_of(i), T.v[:, :]).then_inc(kvsem[i], 16)
+    g.sync.dma_start(T.qs[:, off[rank]:off[rank] + w], T.q[:, 0:w]).then_inc(sem.qin, 16)
+    ve.memset(T.zero[:, 0:n], 0.0).then_inc(sem.zf, 1)
+
+    peers = [T.cores[mem[(i + d) % ns]] for d in range(1, ns)]
+    km = topo.mask(core, peers[0])
+    for p in peers:
+        km &= topo.mask(core, p)
+    nkv = len(_bits(km))
+    g.wait_ge(kvsem[i], 32)
+    g.remote_dma_fused([RemoteDMATransfer(dst_ids=[dst_id(p) for p in peers], dma_engine_mask=km, remote_sem=kvsem[i],
+                                          srcs=[slot], dsts=[slot for _ in peers])], local_sem=sem.sent)
+    sent = nkv
+
+    seq = [(i - d) % ns for d in range(ns)]
+    sp = [T["sp%d" % t] for t in range(ns)]
+
+    def second(t):
+        te.wait_ge(sem["rl%d" % t], 1)
+        te.matmul(T.op[:, 0:n], v_of(seq[t]), T.sr[:, t * NCOL:t * NCOL + n], t == 0, t == ns - 1).then_inc(sem.od, 1)
+
+    nq = sum(Q_ENGINES for _ in order)
+    te.wait_ge(sem.qin, 16 + nq)
+    ve.wait_ge(sem.zf, 1)
+    for t, m in enumerate(seq):
+        te.wait_ge(kvsem[m], 32 if m == i else nkv)
+        te.matmul(sp[t][:, 0:n], k_of(m), T.qs[:, 0:n], True, True).then_inc(sem["s1%d" % t], 1)
+        ve.wait_ge(sem["s1%d" % t], 1)
+        ve.tensor_tensor(T.sr[:, t * NCOL:t * NCOL + n], sp[t][:, 0:n], T.zero[:, 0:n], AluOpType.max).then_inc(sem["rl%d" % t], 1)
+        if t >= 1:
+            second(t - 1)
+    second(ns - 1)
+    ve.wait_ge(sem.od, ns)
+    ve.tensor_copy(T.ys[:, 0:n], T.op[:, 0:n]).then_inc(sem.yr, 1)
+
+    g.sync.wait_ge(sem.yr, 1)
+    g.sync.dma_start(T.y[:, 0:w], T.ys[:, off[rank]:off[rank] + w]).then_inc(sem.st, 16)
+    g.wait_ge(sem.yr, 1)
+    rm = topo.mask(core, T.cores[order[0]])
+    for r in order:
+        rm &= topo.mask(core, T.cores[r])
+    rbits = _bits(rm)
+    for batch in _batches(order, wid, len(rbits)):
+        pad = max(wid[r] for r, _ in batch)
+        trs, e = [], 0
+        for r, ne in batch:
+            trs.append(RemoteDMATransfer(dst_ids=[dst_id(T.cores[r])], dma_engine_mask=_mask(rbits[e:e + ne]), remote_sem=sem.yin,
+                                         srcs=[T.ys[:, off[r]:off[r] + pad]], dsts=[T.ys[:, 0:pad]]))
+            e += ne
+            sent += ne
+        g.remote_dma_fused(trs, local_sem=sem.sent)
+    g.wait_ge(sem.sent, sent)
+    g.sync.wait_ge(sem.st, 16)

@@ -4,6 +4,7 @@ from concourse.mybir import AluOpType
 NCOL = 512
 NMEM = 3
 SLOT = 256
+NBLK = 3
 
 SCRATCH = {
     "kv": ("sbuf", [128, NMEM * SLOT], "bfloat16"),
@@ -13,43 +14,49 @@ SCRATCH = {
     "ys": ("sbuf", [128, NCOL], "bfloat16"),
     "sp0": ("psum", [128, NCOL], "float32"),
     "sp1": ("psum", [128, NCOL], "float32"),
-    "sp2": ("psum", [128, NCOL], "float32"),
-    "op": ("psum", [128, NCOL], "float32"),
+    "sl0": ("psum", [128, NCOL], "float32"),
+    "sl1": ("psum", [128, NCOL], "float32"),
+    "sl2": ("psum", [128, NCOL], "float32"),
+    "op0": ("psum", [128, NCOL], "float32"),
+    "op1": ("psum", [128, NCOL], "float32"),
+    "op2": ("psum", [128, NCOL], "float32"),
 }
-SEMAPHORES = ["kv0", "kv1", "kv2", "qin", "ldq", "sent", "yin", "st", "zf",
-              "s10", "s11", "s12", "rl0", "rl1", "rl2", "od", "yr"]
+SEMAPHORES = ["kv0", "kv1", "kv2", "qin", "ldq", "sent", "yin", "st", "zf", "s10", "s11", "rl0", "rl1",
+              "sl0", "sl1", "sl2", "rr0", "rr1", "rr2", "od0", "od1", "od2", "yr0", "yr1", "yr2"]
 
 Q_ENGINES = 4
 
 
 def _plan(T):
     mem, wid = list(T.tables["MEM"]), list(T.tables["WID"])
-    clients = sorted([r for r in range(len(T.cores)) if r not in mem], key=lambda r: (-wid[r], r))
-    base, extra = divmod(len(clients), len(mem))
-    servers = sorted(mem, key=lambda r: (wid[r], r))
-    plan, p = {}, 0
-    for i, srv in enumerate(servers):
-        size = base + (1 if i >= len(mem) - extra else 0)
-        order = sorted(clients[p:p + size], key=lambda r: (wid[r], r))
+    ns = len(mem)
+    cl = sorted([r for r in range(len(T.cores)) if r not in mem], key=lambda r: (-wid[r], r))
+    rest = sorted(cl[2 * ns:], key=lambda r: (wid[r], r))
+    base, extra = divmod(len(rest), ns)
+    groups, p = [], 0
+    for i in range(ns):
+        size = base + (1 if i < extra else 0)
+        groups.append([rest[p:p + size], sorted(cl[2 * i:2 * i + 2], key=lambda r: (wid[r], r))])
         p += size
+    groups.sort(key=lambda gr: (-sum(wid[r] for b in gr for r in b), -sum(len(b) for b in gr)))
+    plan = {}
+    for srv, gr in zip(sorted(mem, key=lambda r: (wid[r], r)), groups):
+        blocks = [b for b in gr if b] + [[srv]]
         off, c = {}, 0
-        for r in order + [srv]:
-            off[r] = c
-            c += wid[r]
-        assert c <= NCOL
-        plan[srv] = (order, off, c)
+        for b in blocks:
+            for r in b:
+                off[r] = c
+                c += wid[r]
+        assert c <= NCOL and len(blocks) <= NBLK
+        plan[srv] = (blocks, off)
     return plan
 
 
-def _batches(order, wid, neng):
-    out, rest = [], list(order)
-    while rest:
-        b = 1
-        while b * 2 <= min(len(rest), neng):
-            b *= 2
-        out.append([(r, neng // b) for r in rest[len(rest) - b:]])
-        rest = rest[:len(rest) - b]
-    return out
+def _share(neng, b):
+    ne = 1
+    while ne * 2 * b <= neng:
+        ne *= 2
+    return ne
 
 
 def _bits(mask):
@@ -76,8 +83,8 @@ def rank_program(g, core, T, topo):
         return DstId(rid=rid, pnc=pid)
 
     if rank not in mem:
-        srv = [s for s in plan if rank in plan[s][0]][0]
-        order, off, _ = plan[srv]
+        srv = [s for s in plan if rank in plan[s][1]][0]
+        blocks, off = plan[srv]
         sc = T.cores[srv]
         g.sync.dma_start(T.qs[:, 0:w], T.q[:, 0:w]).then_inc(sem.ldq, 16)
         allowed = _bits(topo.mask(core, sc))
@@ -87,15 +94,16 @@ def rank_program(g, core, T, topo):
         g.remote_dma(out_ap=T.qs[:, off[rank]:off[rank] + w], in_ap=T.qs[:, 0:w], remote_sem=sem.qin, local_sem=sem.sent,
                      pid=pid, routing_id=rid, dma_engine_mask=_mask(eng))
         g.wait_ge(sem.sent, len(eng))
-        back = len(_bits(topo.mask(sc, core)))
-        mine = [n for b in _batches(order, wid, back) for (r, n) in b if r == rank][0]
-        g.sync.wait_ge(sem.yin, mine)
+        mine = [b for b in blocks if rank in b][0]
+        g.sync.wait_ge(sem.yin, _share(len(_bits(topo.mask(sc, core))), len(mine)))
         g.sync.dma_start(T.y[:, 0:w], T.ys[:, 0:w]).then_inc(sem.st, 16)
         g.sync.wait_ge(sem.st, 16)
         return
 
-    order, off, n = plan[rank]
-    ns = len(mem)
+    blocks, off = plan[rank]
+    nb, ns = len(blocks), len(mem)
+    cols = [(off[b[0]], off[b[-1]] + wid[b[-1]]) for b in blocks]
+    n = cols[-1][1]
     i = mem.index(rank)
     kvsem = [sem["kv%d" % m] for m in range(ns)]
     te, ve = g.tensor, g.vector
@@ -119,41 +127,67 @@ def rank_program(g, core, T, topo):
     sent = nkv
 
     seq = [(i - d) % ns for d in range(ns)]
-    sp = [T["sp%d" % t] for t in range(ns)]
+    last = ns - 1
+    op = [T["op%d" % b] for b in range(nb)]
 
-    def second(t):
+    def sums(t, b):
+        c0, c1 = cols[b]
+        te.matmul(op[b][:, 0:c1 - c0], v_of(seq[t]), T.sr[:, t * NCOL + c0:t * NCOL + c1], t == 0, t == last).then_inc(sem["od%d" % b], 1)
+
+    def sums_early(t):
         te.wait_ge(sem["rl%d" % t], 1)
-        te.matmul(T.op[:, 0:n], v_of(seq[t]), T.sr[:, t * NCOL:t * NCOL + n], t == 0, t == ns - 1).then_inc(sem.od, 1)
+        for b in range(nb):
+            sums(t, b)
 
-    nq = sum(Q_ENGINES for _ in order)
-    te.wait_ge(sem.qin, 16 + nq)
+    te.wait_ge(sem.qin, 16 + Q_ENGINES * sum(len(b) for b in blocks[:-1]))
     ve.wait_ge(sem.zf, 1)
-    for t, m in enumerate(seq):
-        te.wait_ge(kvsem[m], 32 if m == i else nkv)
-        te.matmul(sp[t][:, 0:n], k_of(m), T.qs[:, 0:n], True, True).then_inc(sem["s1%d" % t], 1)
+    for t in range(last):
+        sp = T["sp%d" % t]
+        te.wait_ge(kvsem[seq[t]], 32 if t == 0 else nkv)
+        te.matmul(sp[:, 0:n], k_of(seq[t]), T.qs[:, 0:n], True, True).then_inc(sem["s1%d" % t], 1)
         ve.wait_ge(sem["s1%d" % t], 1)
-        ve.tensor_tensor(T.sr[:, t * NCOL:t * NCOL + n], sp[t][:, 0:n], T.zero[:, 0:n], AluOpType.max).then_inc(sem["rl%d" % t], 1)
+        ve.tensor_tensor(T.sr[:, t * NCOL:t * NCOL + n], sp[:, 0:n], T.zero[:, 0:n], AluOpType.max).then_inc(sem["rl%d" % t], 1)
         if t >= 1:
-            second(t - 1)
-    second(ns - 1)
-    ve.wait_ge(sem.od, ns)
-    ve.tensor_copy(T.ys[:, 0:n], T.op[:, 0:n]).then_inc(sem.yr, 1)
+            sums_early(t - 1)
 
-    g.sync.wait_ge(sem.yr, 1)
-    g.sync.dma_start(T.y[:, 0:w], T.ys[:, off[rank]:off[rank] + w]).then_inc(sem.st, 16)
-    g.wait_ge(sem.yr, 1)
-    rm = topo.mask(core, T.cores[order[0]])
-    for r in order:
-        rm &= topo.mask(core, T.cores[r])
-    rbits = _bits(rm)
-    for batch in _batches(order, wid, len(rbits)):
-        pad = max(wid[r] for r, _ in batch)
-        trs, e = [], 0
-        for r, ne in batch:
-            trs.append(RemoteDMATransfer(dst_ids=[dst_id(T.cores[r])], dma_engine_mask=_mask(rbits[e:e + ne]), remote_sem=sem.yin,
-                                         srcs=[T.ys[:, off[r]:off[r] + pad]], dsts=[T.ys[:, 0:pad]]))
-            e += ne
-            sent += ne
+    def score_l(b):
+        c0, c1 = cols[b]
+        te.matmul(T["sl%d" % b][:, 0:c1 - c0], k_of(seq[last]), T.qs[:, c0:c1], True, True).then_inc(sem["sl%d" % b], 1)
+
+    def clamp_l(b):
+        c0, c1 = cols[b]
+        ve.wait_ge(sem["sl%d" % b], 1)
+        ve.tensor_tensor(T.sr[:, last * NCOL + c0:last * NCOL + c1], T["sl%d" % b][:, 0:c1 - c0], T.zero[:, 0:c1 - c0],
+                         AluOpType.max).then_inc(sem["rr%d" % b], 1)
+
+    te.wait_ge(kvsem[seq[last]], nkv)
+    for b in range(min(2, nb)):
+        score_l(b)
+        clamp_l(b)
+    sums_early(last - 1)
+    for b in range(nb):
+        c0, c1 = cols[b]
+        te.wait_ge(sem["rr%d" % b], 1)
+        sums(last, b)
+        ve.wait_ge(sem["od%d" % b], ns)
+        ve.tensor_copy(T.ys[:, c0:c1], op[b][:, 0:c1 - c0]).then_inc(sem["yr%d" % b], 1)
+        if b + 2 < nb:
+            score_l(b + 2)
+            clamp_l(b + 2)
+
+    for b in range(nb - 1):
+        rm = topo.mask(core, T.cores[blocks[b][0]])
+        for r in blocks[b]:
+            rm &= topo.mask(core, T.cores[r])
+        rbits = _bits(rm)
+        ne = _share(len(rbits), len(blocks[b]))
+        pad = max(wid[r] for r in blocks[b])
+        trs = [RemoteDMATransfer(dst_ids=[dst_id(T.cores[r])], dma_engine_mask=_mask(rbits[x * ne:(x + 1) * ne]), remote_sem=sem.yin,
+                                 srcs=[T.ys[:, off[r]:off[r] + pad]], dsts=[T.ys[:, 0:pad]]) for x, r in enumerate(blocks[b])]
+        g.wait_ge(sem["yr%d" % b], 1)
         g.remote_dma_fused(trs, local_sem=sem.sent)
+        sent += ne * len(trs)
+    g.sync.wait_ge(sem["yr%d" % (nb - 1)], 1)
+    g.sync.dma_start(T.y[:, 0:w], T.ys[:, off[rank]:off[rank] + w]).then_inc(sem.st, 16)
     g.wait_ge(sem.sent, sent)
     g.sync.wait_ge(sem.st, 16)

from concourse.bass import DstId, RemoteDMATransfer
from concourse.mybir import AluOpType

NCOL = 512
NMEM = 3
SLOT = 256
NBLK = 3

SCRATCH = {
    "kv": ("sbuf", [128, NMEM * SLOT], "bfloat16"),
    "qs": ("sbuf", [128, NCOL], "bfloat16"),
    "zero": ("sbuf", [128, NCOL], "float32"),
    "sr": ("sbuf", [128, NMEM * NCOL], "bfloat16"),
    "ys": ("sbuf", [128, NCOL], "bfloat16"),
    "sp0": ("psum", [128, NCOL], "float32"),
    "sp1": ("psum", [128, NCOL], "float32"),
    "sl0": ("psum", [128, NCOL], "float32"),
    "sl1": ("psum", [128, NCOL], "float32"),
    "sl2": ("psum", [128, NCOL], "float32"),
    "op0": ("psum", [128, NCOL], "float32"),
    "op1": ("psum", [128, NCOL], "float32"),
    "op2": ("psum", [128, NCOL], "float32"),
}
SEMAPHORES = ["kv0", "kv1", "kv2", "qin", "ldq", "sent", "yin", "st", "zf", "s10", "s11", "rl0", "rl1",
              "sl0", "sl1", "sl2", "rr0", "rr1", "rr2", "od0", "od1", "od2", "yr0", "yr1", "yr2"]

Q_ENGINES = 4


def _plan(T):
    mem, wid = list(T.tables["MEM"]), list(T.tables["WID"])
    ns = len(mem)
    cl = sorted([r for r in range(len(T.cores)) if r not in mem], key=lambda r: (-wid[r], r))
    rest = sorted(cl[2 * ns:], key=lambda r: (wid[r], r))
    base, extra = divmod(len(rest), ns)
    groups, p = [], 0
    for i in range(ns):
        size = base + (1 if i < extra else 0)
        groups.append([rest[p:p + size], sorted(cl[2 * i:2 * i + 2], key=lambda r: (wid[r], r))])
        p += size
    groups.sort(key=lambda gr: (-sum(wid[r] for b in gr for r in b), -sum(len(b) for b in gr)))
    plan = {}
    for srv, gr in zip(sorted(mem, key=lambda r: (wid[r], r)), groups):
        blocks = [b for b in gr if b] + [[srv]]
        off, c = {}, 0
        for b in blocks:
            for r in b:
                off[r] = c
                c += wid[r]
        assert c <= NCOL and len(blocks) <= NBLK
        plan[srv] = (blocks, off)
    return plan


def _share(neng, b):
    ne = 1
    while ne * 2 * b <= neng:
        ne *= 2
    return ne


def _bits(mask):
    return [e for e in range(16) if (mask >> e) & 1]


def _mask(bits):
    m = 0
    for e in bits:
        m |= 1 << e
    return m


def rank_program(g, core, T, topo):
    rank = T.rank_of(core)
    if rank is None:
        return
    mem, wid, sem = list(T.tables["MEM"]), list(T.tables["WID"]), T.sem
    plan = _plan(T)
    w = wid[rank]

    def dst_id(d):
        rid, pid = topo.addr(d, core)
        return DstId(rid=rid, pnc=pid)

    if rank not in mem:
        srv = [s for s in plan if rank in plan[s][1]][0]
        blocks, off = plan[srv]
        sc = T.cores[srv]
        g.sync.dma_start(T.qs[:, 0:w], T.q[:, 0:w]).then_inc(sem.ldq, 16)
        allowed = _bits(topo.mask(core, sc))
        eng = allowed[::len(allowed) // Q_ENGINES][:Q_ENGINES]
        rid, pid = topo.addr(sc, core)
        g.wait_ge(sem.ldq, 16)
        g.remote_dma(out_ap=T.qs[:, off[rank]:off[rank] + w], in_ap=T.qs[:, 0:w], remote_sem=sem.qin, local_sem=sem.sent,
                     pid=pid, routing_id=rid, dma_engine_mask=_mask(eng))
        g.wait_ge(sem.sent, len(eng))
        mine = [b for b in blocks if rank in b][0]
        g.sync.wait_ge(sem.yin, _share(len(_bits(topo.mask(sc, core))), len(mine)))
        g.sync.dma_start(T.y[:, 0:w], T.ys[:, 0:w]).then_inc(sem.st, 16)
        g.sync.wait_ge(sem.st, 16)
        return

    blocks, off = plan[rank]
    nb, ns = len(blocks), len(mem)
    cols = [(off[b[0]], off[b[-1]] + wid[b[-1]]) for b in blocks]
    n = cols[-1][1]
    i = mem.index(rank)
    kvsem = [sem["kv%d" % m] for m in range(ns)]
    te, ve = g.tensor, g.vector
    k_of = lambda m: T.kv[:, m * SLOT:m * SLOT + 128]
    v_of = lambda m: T.kv[:, m * SLOT + 128:(m + 1) * SLOT]
    slot = T.kv[:, i * SLOT:(i + 1) * SLOT]

    g.sync.dma_start(k_of(i), T.k[:, :]).then_inc(kvsem[i], 16)
    g.scalar.dma_start(v_of(i), T.v[:, :]).then_inc(kvsem[i], 16)
    g.sync.dma_start(T.qs[:, off[rank]:off[rank] + w], T.q[:, 0:w]).then_inc(sem.qin, 16)
    ve.memset(T.zero[:, 0:n], 0.0).then_inc(sem.zf, 1)

    peers = [T.cores[mem[(i + d) % ns]] for d in range(1, ns)]
    km = topo.mask(core, peers[0])
    for p in peers:
        km &= topo.mask(core, p)
    nkv = len(_bits(km))
    g.wait_ge(kvsem[i], 32)
    g.remote_dma_fused([RemoteDMATransfer(dst_ids=[dst_id(p) for p in peers], dma_engine_mask=km, remote_sem=kvsem[i],
                                          srcs=[slot], dsts=[slot for _ in peers])], local_sem=sem.sent)
    sent = nkv

    seq = [(i - d) % ns for d in range(ns)]
    last = ns - 1
    op = [T["op%d" % b] for b in range(nb)]

    def sums(t, b):
        c0, c1 = cols[b]
        te.matmul(op[b][:, 0:c1 - c0], v_of(seq[t]), T.sr[:, t * NCOL + c0:t * NCOL + c1], t == 0, t == last).then_inc(sem["od%d" % b], 1)

    def sums_early(t):
        te.wait_ge(sem["rl%d" % t], 1)
        for b in range(nb):
            sums(t, b)

    te.wait_ge(sem.qin, 16 + Q_ENGINES * sum(len(b) for b in blocks[:-1]))
    ve.wait_ge(sem.zf, 1)
    for t in range(last):
        sp = T["sp%d" % t]
        te.wait_ge(kvsem[seq[t]], 32 if t == 0 else nkv)
        te.matmul(sp[:, 0:n], k_of(seq[t]), T.qs[:, 0:n], True, True).then_inc(sem["s1%d" % t], 1)
        ve.wait_ge(sem["s1%d" % t], 1)
        ve.tensor_tensor(T.sr[:, t * NCOL:t * NCOL + n], sp[:, 0:n], T.zero[:, 0:n], AluOpType.max).then_inc(sem["rl%d" % t], 1)
        if t >= 1:
            sums_early(t - 1)

    def score_l(b):
        c0, c1 = cols[b]
        te.matmul(T["sl%d" % b][:, 0:c1 - c0], k_of(seq[last]), T.qs[:, c0:c1], True, True).then_inc(sem["sl%d" % b], 1)

    def clamp_l(b):
        c0, c1 = cols[b]
        ve.wait_ge(sem["sl%d" % b], 1)
        ve.tensor_tensor(T.sr[:, last * NCOL + c0:last * NCOL + c1], T["sl%d" % b][:, 0:c1 - c0], T.zero[:, 0:c1 - c0],
                         AluOpType.max).then_inc(sem["rr%d" % b], 1)

    te.wait_ge(kvsem[seq[last]], nkv)
    for b in range(min(2, nb)):
        score_l(b)
        clamp_l(b)
    sums_early(last - 1)
    for b in range(nb):
        c0, c1 = cols[b]
        te.wait_ge(sem["rr%d" % b], 1)
        sums(last, b)
        ve.wait_ge(sem["od%d" % b], ns)
        ve.tensor_copy(T.ys[:, c0:c1], op[b][:, 0:c1 - c0]).then_inc(sem["yr%d" % b], 1)
        if b + 2 < nb:
            score_l(b + 2)
            clamp_l(b + 2)

    for b in range(nb - 1):
        rm = topo.mask(core, T.cores[blocks[b][0]])
        for r in blocks[b]:
            rm &= topo.mask(core, T.cores[r])
        rbits = _bits(rm)
        ne = _share(len(rbits), len(blocks[b]))
        pad = max(wid[r] for r in blocks[b])
        trs = [RemoteDMATransfer(dst_ids=[dst_id(T.cores[r])], dma_engine_mask=_mask(rbits[x * ne:(x + 1) * ne]), remote_sem=sem.yin,
                                 srcs=[T.ys[:, off[r]:off[r] + pad]], dsts=[T.ys[:, 0:pad]]) for x, r in enumerate(blocks[b])]
        g.wait_ge(sem["yr%d" % b], 1)
        g.remote_dma_fused(trs, local_sem=sem.sent)
        sent += ne * len(trs)
    g.sync.wait_ge(sem["yr%d" % (nb - 1)], 1)
    g.sync.dma_start(T.y[:, 0:w], T.ys[:, off[rank]:off[rank] + w]).then_inc(sem.st, 16)
    g.wait_ge(sem.sent, sent)
    g.sync.wait_ge(sem.st, 16)
